import numpy as np
import ml_dtypes


def mxq(x, axis, fmt="e4m3"):
    dtype, down = {"e4m3": (ml_dtypes.float8_e4m3fn, 7), "e5m2": (ml_dtypes.float8_e5m2, 14)}[fmt]
    v = np.moveaxis(np.asarray(x, np.float32).astype(ml_dtypes.bfloat16).astype(np.float64), axis, -1)
    blocks = v.reshape(v.shape[:-1] + (-1, 32))
    amax = np.abs(blocks).max(-1, keepdims=True)
    byte = np.maximum(np.where(amax > 0, np.frexp(amax)[1] - 1 + 127, 0) - down, 1)
    scale = np.exp2(byte - 127.0)
    codes = (blocks / scale).astype(np.float32).astype(dtype).astype(np.float64)
    return np.moveaxis((codes * scale).reshape(v.shape), -1, axis)


WIDE = False


def mx_kscale(k):
    if not WIDE:
        return np.ones(k)
    levels = np.array([30, -30])
    if k % 512:
        return np.exp2(np.random.permutation(np.resize(levels, k // 32))).repeat(32)
    a = np.empty((k // 512, 16))
    for p in range(k // 512):
        a[p, :8] = np.random.permutation(np.resize(levels, 8))
        for g in range(8):
            far = levels[np.abs(levels - a[p, g]) >= 10]
            a[p, g + 8] = far[np.random.randint(len(far))]
    return np.exp2(a.ravel()).repeat(32)


def f64(x):
    return np.asarray(x).astype(np.float64)


def striped(idx):
    return np.tile(np.asarray(idx).reshape(-1, 16).T, (8, 1)).astype(np.uint16)


def unstriped(offs):
    return offs[:16].T.reshape(-1).astype(np.int64)


E2M1 = np.array([0.0, 0.5, 1.0, 1.5, 2.0, 3.0, 4.0, 6.0, -0.0, -0.5, -1.0, -1.5, -2.0, -3.0, -4.0, -6.0])


def pack_weight(w, fmt):
    k, n = w.shape
    w = f64(np.asarray(w, np.float32).astype(ml_dtypes.bfloat16)).reshape(k // 32, 32, n)
    amax = np.abs(w).max(1)
    if fmt == "e4m3":
        byte = np.frexp(amax)[1] - 1 + 127 - 7
    else:
        mant, ex = np.frexp(amax / 6.0)
        byte = np.where(mant > 0.5, ex, ex - 1) + 127
    byte = np.clip(np.where(amax > 0, byte, 1), 1, 254)
    scaled = (w * np.exp2(127.0 - byte)[:, None, :]).reshape(k, n).astype(np.float32)
    by_word = np.ascontiguousarray(scaled.reshape(k // 512, 128, 4, n).transpose(0, 1, 3, 2))
    if fmt == "e4m3":
        words = by_word.astype(ml_dtypes.float8_e4m3fn).view(np.uint8)
    else:
        c = by_word.astype(ml_dtypes.float4_e2m1fn).view(np.uint8) & 0xF
        words = (c[..., 0::2] | (c[..., 1::2] << 4)).reshape(k // 512, 128, 2 * n)
    return np.ascontiguousarray(words), np.ascontiguousarray(byte.astype(np.uint8).reshape(k // 512, 16, n))


def unpack_weight(words, scales, fmt):
    g, _, n = scales.shape
    words = np.ascontiguousarray(words).reshape(g, 128, n, -1)
    if fmt == "e4m3":
        vals = words.view(ml_dtypes.float8_e4m3fn).astype(np.float64)
    else:
        nib = np.empty((g, 128, n, 4), np.uint8)
        nib[..., 0::2] = words & 0xF
        nib[..., 1::2] = words >> 4
        vals = E2M1[nib]
    vals = vals * np.repeat(np.exp2(scales.astype(np.float64) - 127.0), 8, axis=1)[..., None]
    return vals.transpose(0, 1, 3, 2).reshape(g * 512, n)


K, N, T, J = 512, 512, 2048, 512


def setup_inputs():
    n = np.random.standard_normal
    idx = np.random.permutation(T)[:J]
    fk = mx_kscale(K)
    fn = mx_kscale(N)
    xtp = pack_weight(n((K, T)) / fk[:, None], "e4m3")
    wp = pack_weight(n((K, N)) * 1 / np.sqrt(K) * fk[:, None], "e2m1")
    wtp = pack_weight(n((N, K)) * 1 / np.sqrt(N) / fn[:, None], "e4m3")
    return {
        "xt_words": xtp[0],
        "xt_scales": xtp[1],
        "w_words": wp[0],
        "w_scales": wp[1],
        "tea": (np.random.uniform(-0.9, 0.9, (N, T))).astype(np.float32),
        "us": (np.random.uniform(0.5, 2.0, (N, 1)) * fn[:, None]).astype(np.float32),
        "wt_words": wtp[0],
        "wt_scales": wtp[1],
        "res": (0.3 * n((K, J))).astype(np.float32),
        "offs": striped(idx),
    }


def reference(xt_words, xt_scales, w_words, w_scales, tea, us, wt_words, wt_scales, res, offs):
    idx = unstriped(offs)
    xtu = unpack_weight(xt_words, xt_scales, "e4m3")
    wu = unpack_weight(w_words, w_scales, "e2m1")
    wtu = unpack_weight(wt_words, wt_scales, "e4m3")
    xtidxg = xtu[:, idx]
    z = wu.T @ xtidxg
    d = (np.tanh(z) - f64(tea)[:, idx]) * f64(us)
    dq = mxq(d, 0, "e5m2")
    dx = wtu.T @ dq
    y = dx + f64(res)
    return y

@@ -1,0 +1,127 @@
+from contextlib import ExitStack
+
+import concourse.mybir as mybir
+
+K, N, T, J = 512, 512, 2048, 512
+FLOPS = 2 * 2 * K * N * J
+
+F32 = mybir.dt.float32
+BF16 = mybir.dt.bfloat16
+I32 = mybir.dt.int32
+U32 = mybir.dt.uint32
+U16 = mybir.dt.uint16
+U8 = mybir.dt.uint8
+E4M3 = mybir.dt.float8_e4m3fn_x4
+E5M2 = mybir.dt.float8_e5m2_x4
+E2M1 = mybir.dt.float4_e2m1fn_x4
+ACT = mybir.ActivationFunctionType
+ALU = mybir.AluOpType
+
+P = 128
+PACK = 4
+
+
+def load_scale_rows(queue, plane, rows):
+    for q in range(4):
+        queue.dma_start(out=plane[32 * q : 32 * q + 4, :].bitcast(I32), in_=rows[4 * q : 4 * q + 4, :].bitcast(I32))
+
+
+def tile_list_feature_match_back_kernel(
+    tc, xt_words, xt_scales, w_words, w_scales, tea, us, wt_words, wt_scales, res, offs, out
+):
+    nc = tc.nc
+    with ExitStack() as ctx:
+        keep = ctx.enter_context(tc.tile_pool(name="keep", bufs=1))
+        psum = ctx.enter_context(tc.psum_pool(name="psum", bufs=1))
+
+        offsets = keep.tile([P, J // 16], U16, name="offsets")
+        w_raw = keep.tile([P, 2 * N], U8, name="w_raw", align_bytes=64)
+        ws_raw = keep.tile([P, N], U8, name="ws_raw", align_bytes=64)
+        x_all = keep.tile([P, T], I32, name="x_all", align_bytes=64)
+        xs_all = keep.tile([P, T], U8, name="xs_all", align_bytes=64)
+        wt_codes = keep.tile([P, K], I32, name="wt_codes", align_bytes=64)
+        wt_plane = keep.tile([P, K], U8, name="wt_plane", align_bytes=64)
+        us_sb = keep.tile([P, PACK], F32, name="us_sb")
+        res_sb = keep.tile([P, PACK, J], F32, name="res_sb")
+        tea_sb = [keep.tile([P, T], F32, name=f"tea{t}") for t in range(PACK)]
+        warm = keep.tile([P, 1], F32, name="warm")
+        warm2 = keep.tile([P, 1], F32, name="warm2")
+
+        nc.vector.memset(ws_raw[:].bitcast(I32), 0)
+        nc.vector.memset(xs_all[:].bitcast(I32), 0)
+        nc.gpsimd.memset(warm[:], 0.0)
+        nc.gpsimd.memset(wt_plane[:].bitcast(I32), 0)
+
+        tea_rows = tea.rearrange("(p t) c -> t p c", t=PACK)
+        nc.sync.dma_start(offsets[:], offs)
+        nc.sync.dma_start(out=w_raw[:].bitcast(I32), in_=w_words[0].bitcast(I32))
+        load_scale_rows(nc.sync, ws_raw, w_scales[0])
+        nc.sync.dma_start(out=x_all[:], in_=xt_words[0].rearrange("p c r -> p (c r)").bitcast(I32))
+        nc.sync.dma_start(out=tea_sb[0][:], in_=tea_rows[0])
+        load_scale_rows(nc.scalar, xs_all, xt_scales[0])
+        nc.scalar.dma_start(out=us_sb[:], in_=us.rearrange("(p t) o -> p (t o)", t=PACK))
+        nc.scalar.activation(warm2[:], warm[:], ACT.Tanh)
+        for t in range(1, PACK):
+            nc.sync.dma_start(out=tea_sb[t][:], in_=tea_rows[t])
+        load_scale_rows(nc.gpsimd, wt_plane, wt_scales[0])
+        nc.sync.dma_start(out=wt_codes[:], in_=wt_words[0].rearrange("p c r -> p (c r)").bitcast(I32))
+        nc.sync.dma_start(out=res_sb[:], in_=res.rearrange("(b p) j -> p b j", p=P))
+
+        w_codes = keep.tile([P, 2 * N], U8, name="w_codes", align_bytes=64)
+        w_plane = keep.tile([P, N], U8, name="w_plane", align_bytes=64)
+        nc.vector.tensor_copy(
+            out=w_codes[:].rearrange("p (t m b) -> p t m b", t=PACK, b=2),
+            in_=w_raw[:].rearrange("p (m t b) -> p t m b", t=PACK, b=2),
+        )
+        nc.vector.tensor_copy(
+            out=w_plane[:].rearrange("p (t m) -> p t m", t=PACK),
+            in_=ws_raw[:].rearrange("p (m t) -> p t m", t=PACK),
+        )
+        x_codes = keep.tile([P, J], U32, name="x_codes", align_bytes=64)
+        x_plane = keep.tile([P, J], U8, name="x_plane", align_bytes=64)
+        nc.vector.tensor_copy(x_plane[:], xs_all[:].indirect(offsets[:]))
+        nc.vector.tensor_copy(x_codes[:], x_all[:].bitcast(U32).indirect(offsets[:]))
+        neg_us = keep.tile([P, PACK], F32, name="neg_us")
+        nc.gpsimd.tensor_scalar(neg_us[:], us_sb[:], -1.0, 0.0, ALU.mult, ALU.add)
+
+        d_bf = keep.tile([P, J, PACK], BF16, name="d_bf", align_bytes=64)
+        for t in range(PACK):
+            z = psum.tile([P, J], F32, name=f"z{t}")
+            nc.tensor.matmul_mx(
+                out=z[:],
+                lhsT=w_codes[:, 2 * P * t : 2 * P * (t + 1)].bitcast(E2M1),
+                lhsT_scale=w_plane[:, P * t : P * (t + 1)],
+                rhs=x_codes[:].bitcast(E4M3),
+                rhs_scale=x_plane[:],
+                start=True,
+                stop=True,
+            )
+            th = keep.tile([P, J], F32, name=f"th{t}")
+            nc.scalar.activation(th[:], z[:], ACT.Tanh)
+            diff = keep.tile([P, J], F32, name=f"diff{t}")
+            nc.vector.tensor_tensor(diff[:], tea_sb[t][:].indirect(offsets[:]), th[:], ALU.subtract)
+            if t < 2:
+                nc.scalar.activation(d_bf[:, :, t], diff[:], ACT.Copy, scale=neg_us[:, t : t + 1])
+            else:
+                nc.vector.tensor_scalar(d_bf[:, :, t], diff[:], neg_us[:, t : t + 1], None, ALU.mult)
+
+        d_codes = keep.tile([P, J], U32, name="d_codes", align_bytes=64)
+        d_plane = keep.tile([P, J], U8, name="d_plane", align_bytes=64)
+        nc.vector.quantize_mx(
+            out=d_codes[:].bitcast(E5M2), scales=d_plane[:], in_=d_bf[:].rearrange("p j t -> p (j t)")
+        )
+        for b in range(PACK):
+            dx = psum.tile([P, J], F32, name=f"dx{b}")
+            nc.tensor.matmul_mx(
+                out=dx[:],
+                lhsT=wt_codes[:, P * b : P * (b + 1)].bitcast(E4M3),
+                lhsT_scale=wt_plane[:, P * b : P * (b + 1)],
+                rhs=d_codes[:].bitcast(E5M2),
+                rhs_scale=d_plane[:],
+                start=True,
+                stop=True,
+            )
+            y = keep.tile([P, J], F32, name=f"y{b}")
+            nc.vector.tensor_tensor(y[:], dx[:], res_sb[:, b, :], ALU.add)
+            queue = nc.sync if b % 2 == 0 else nc.scalar
+            queue.dma_start(out=out[P * b : P * (b + 1), :], in_=y[:])

@@ -19,6 +19,7 @@ ALU = mybir.AluOpType
 
 P = 128
 PACK = 4
+HALF = J // 2
 
 
 def load_scale_rows(queue, plane, rows):
@@ -32,59 +33,57 @@ def tile_list_feature_match_back_kernel(
     nc = tc.nc
     with ExitStack() as ctx:
         keep = ctx.enter_context(tc.tile_pool(name="keep", bufs=1))
+        ring = ctx.enter_context(tc.tile_pool(name="ring", bufs=4))
         psum = ctx.enter_context(tc.psum_pool(name="psum", bufs=1))
 
         offsets = keep.tile([P, J // 16], U16, name="offsets")
         w_raw = keep.tile([P, 2 * N], U8, name="w_raw", align_bytes=64)
         ws_raw = keep.tile([P, N], U8, name="ws_raw", align_bytes=64)
-        x_all = keep.tile([P, T], I32, name="x_all", align_bytes=64)
         xs_all = keep.tile([P, T], U8, name="xs_all", align_bytes=64)
-        wt_codes = keep.tile([P, K], I32, name="wt_codes", align_bytes=64)
         wt_plane = keep.tile([P, K], U8, name="wt_plane", align_bytes=64)
         us_sb = keep.tile([P, PACK], F32, name="us_sb")
-        res_sb = keep.tile([P, PACK, J], F32, name="res_sb")
-        tea_sb = [keep.tile([P, T], F32, name=f"tea{t}") for t in range(PACK)]
         warm = keep.tile([P, 1], F32, name="warm")
         warm2 = keep.tile([P, 1], F32, name="warm2")
 
-        nc.vector.memset(ws_raw[:].bitcast(I32), 0)
+        nc.gpsimd.memset(ws_raw[:].bitcast(I32), 0)
         nc.vector.memset(xs_all[:].bitcast(I32), 0)
-        nc.gpsimd.memset(warm[:], 0.0)
-        nc.gpsimd.memset(wt_plane[:].bitcast(I32), 0)
+        nc.vector.memset(warm[:], 0.0)
 
         tea_rows = tea.rearrange("(p t) c -> t p c", t=PACK)
         nc.sync.dma_start(offsets[:], offs)
         nc.sync.dma_start(out=w_raw[:].bitcast(I32), in_=w_words[0].bitcast(I32))
-        load_scale_rows(nc.sync, ws_raw, w_scales[0])
-        nc.sync.dma_start(out=x_all[:], in_=xt_words[0].rearrange("p c r -> p (c r)").bitcast(I32))
-        nc.sync.dma_start(out=tea_sb[0][:], in_=tea_rows[0])
         load_scale_rows(nc.scalar, xs_all, xt_scales[0])
-        nc.scalar.dma_start(out=us_sb[:], in_=us.rearrange("(p t) o -> p (t o)", t=PACK))
-        nc.scalar.activation(warm2[:], warm[:], ACT.Tanh)
-        for t in range(1, PACK):
-            nc.sync.dma_start(out=tea_sb[t][:], in_=tea_rows[t])
+        load_scale_rows(nc.gpsimd, ws_raw, w_scales[0])
+        nc.gpsimd.dma_start(out=us_sb[:], in_=us.rearrange("(p t) o -> p (t o)", t=PACK))
         load_scale_rows(nc.gpsimd, wt_plane, wt_scales[0])
-        nc.sync.dma_start(out=wt_codes[:], in_=wt_words[0].rearrange("p c r -> p (c r)").bitcast(I32))
-        nc.sync.dma_start(out=res_sb[:], in_=res.rearrange("(b p) j -> p b j", p=P))
+        nc.scalar.activation(warm2[:], warm[:], ACT.Tanh)
+        x_all = ring.tile([P, T], I32, name="x_all", tag="big", align_bytes=64)
+        nc.sync.dma_start(out=x_all[:], in_=xt_words[0].rearrange("p c r -> p (c r)").bitcast(I32))
+        tea_sb = []
+        for t in range(PACK - 1):
+            tea_sb.append(ring.tile([P, T], F32, name=f"tea{t}", tag="big", align_bytes=64))
+            nc.sync.dma_start(out=tea_sb[t][:], in_=tea_rows[t])
 
         w_codes = keep.tile([P, 2 * N], U8, name="w_codes", align_bytes=64)
         w_plane = keep.tile([P, N], U8, name="w_plane", align_bytes=64)
         nc.vector.tensor_copy(
-            out=w_codes[:].rearrange("p (t m b) -> p t m b", t=PACK, b=2),
-            in_=w_raw[:].rearrange("p (m t b) -> p t m b", t=PACK, b=2),
-        )
-        nc.vector.tensor_copy(
-            out=w_plane[:].rearrange("p (t m) -> p t m", t=PACK),
-            in_=ws_raw[:].rearrange("p (m t) -> p t m", t=PACK),
+            out=w_codes[:].bitcast(U16).rearrange("p (t m) -> p t m", t=PACK),
+            in_=w_raw[:].bitcast(U16).rearrange("p (m t) -> p t m", t=PACK),
         )
         x_codes = keep.tile([P, J], U32, name="x_codes", align_bytes=64)
         x_plane = keep.tile([P, J], U8, name="x_plane", align_bytes=64)
-        nc.vector.tensor_copy(x_plane[:], xs_all[:].indirect(offsets[:]))
         nc.vector.tensor_copy(x_codes[:], x_all[:].bitcast(U32).indirect(offsets[:]))
+        nc.vector.tensor_copy(x_plane[:], xs_all[:].indirect(offsets[:]))
+        ws_by_slot = ws_raw[:].rearrange("p (m t) -> p t m", t=PACK)
+        for t in range(PACK):
+            nc.vector.tensor_copy(out=w_plane[:, P * t : P * (t + 1)], in_=ws_by_slot[:, t, :])
+        tea_sb.append(ring.tile([P, T], F32, name="tea3", tag="big", align_bytes=64))
+        nc.sync.dma_start(out=tea_sb[3][:], in_=tea_rows[3])
         neg_us = keep.tile([P, PACK], F32, name="neg_us")
         nc.gpsimd.tensor_scalar(neg_us[:], us_sb[:], -1.0, 0.0, ALU.mult, ALU.add)
 
-        d_bf = keep.tile([P, J, PACK], BF16, name="d_bf", align_bytes=64)
+        d_lo = keep.tile([P, HALF, PACK], BF16, name="d_lo", align_bytes=64)
+        d_hi = keep.tile([P, HALF, PACK], BF16, name="d_hi", align_bytes=64)
         for t in range(PACK):
             z = psum.tile([P, J], F32, name=f"z{t}")
             nc.tensor.matmul_mx(
@@ -98,18 +97,30 @@ def tile_list_feature_match_back_kernel(
             )
             th = keep.tile([P, J], F32, name=f"th{t}")
             nc.scalar.activation(th[:], z[:], ACT.Tanh)
+            cuts = [0, J] if t < PACK - 1 else [0, HALF, HALF + HALF // 2, J]
             diff = keep.tile([P, J], F32, name=f"diff{t}")
-            nc.vector.tensor_tensor(diff[:], tea_sb[t][:].indirect(offsets[:]), th[:], ALU.subtract)
-            if t < 2:
-                nc.scalar.activation(d_bf[:, :, t], diff[:], ACT.Copy, scale=neg_us[:, t : t + 1])
-            else:
-                nc.vector.tensor_scalar(d_bf[:, :, t], diff[:], neg_us[:, t : t + 1], None, ALU.mult)
+            for lo, hi in zip(cuts, cuts[1:]):
+                picked = tea_sb[t][:].indirect(offsets[:, lo // 16 : hi // 16])
+                nc.vector.tensor_tensor(diff[:, lo:hi], picked, th[:, lo:hi], ALU.subtract)
+            if t == 0:
+                wt_codes = ring.tile([P, K], I32, name="wt_codes", tag="big", align_bytes=64)
+                nc.sync.dma_start(out=wt_codes[:], in_=wt_words[0].rearrange("p c r -> p (c r)").bitcast(I32))
+            if t == 1:
+                res_sb = ring.tile([P, PACK, J], F32, name="res_sb", tag="big", align_bytes=64)
+                nc.sync.dma_start(out=res_sb[:], in_=res.rearrange("(b p) j -> p b j", p=P))
+            factor = neg_us[:, t : t + 1]
+            nc.scalar.activation(d_lo[:, :, t], diff[:, :HALF], ACT.Copy, scale=factor)
+            cuts = [HALF, J] if t < PACK - 1 else cuts[1:]
+            for lo, hi in zip(cuts, cuts[1:]):
+                nc.vector.tensor_scalar(d_hi[:, lo - HALF : hi - HALF, t], diff[:, lo:hi], factor, None, ALU.mult)
 
         d_codes = keep.tile([P, J], U32, name="d_codes", align_bytes=64)
         d_plane = keep.tile([P, J], U8, name="d_plane", align_bytes=64)
-        nc.vector.quantize_mx(
-            out=d_codes[:].bitcast(E5M2), scales=d_plane[:], in_=d_bf[:].rearrange("p j t -> p (j t)")
-        )
+        for h, d_half in enumerate((d_lo, d_hi)):
+            cols = slice(HALF * h, HALF * (h + 1))
+            nc.vector.quantize_mx(
+                out=d_codes[:, cols].bitcast(E5M2), scales=d_plane[:, cols], in_=d_half[:].rearrange("p j t -> p (j t)")
+            )
         for b in range(PACK):
             dx = psum.tile([P, J], F32, name=f"dx{b}")
             nc.tensor.matmul_mx(
@@ -122,6 +133,8 @@ def tile_list_feature_match_back_kernel(
                 stop=True,
             )
             y = keep.tile([P, J], F32, name=f"y{b}")
-            nc.vector.tensor_tensor(y[:], dx[:], res_sb[:, b, :], ALU.add)
-            queue = nc.sync if b % 2 == 0 else nc.scalar
-            queue.dma_start(out=out[P * b : P * (b + 1), :], in_=y[:])
+            cuts = [0, J] if b < PACK - 1 else [0, HALF, J]
+            for i, (lo, hi) in enumerate(zip(cuts, cuts[1:])):
+                nc.vector.tensor_tensor(y[:, lo:hi], dx[:, lo:hi], res_sb[:, b, lo:hi], ALU.add)
+                queue = nc.sync if (b + i) % 2 == 0 else nc.scalar
+                queue.dma_start(out=out[P * b : P * (b + 1), lo:hi], in_=y[:, lo:hi])

@@ -20,11 +20,12 @@ ALU = mybir.AluOpType
 P = 128
 PACK = 4
 HALF = J // 2
+QUARTER = J // 4
 
 
-def load_scale_rows(queue, plane, rows):
+def load_scale_rows(nc, plane, rows):
     for q in range(4):
-        queue.dma_start(out=plane[32 * q : 32 * q + 4, :].bitcast(I32), in_=rows[4 * q : 4 * q + 4, :].bitcast(I32))
+        nc.sync.dma_start(out=plane[32 * q : 32 * q + 4, :].bitcast(I32), in_=rows[4 * q : 4 * q + 4, :].bitcast(I32))
 
 
 def tile_list_feature_match_back_kernel(
@@ -33,7 +34,6 @@ def tile_list_feature_match_back_kernel(
     nc = tc.nc
     with ExitStack() as ctx:
         keep = ctx.enter_context(tc.tile_pool(name="keep", bufs=1))
-        ring = ctx.enter_context(tc.tile_pool(name="ring", bufs=4))
         psum = ctx.enter_context(tc.psum_pool(name="psum", bufs=1))
 
         offsets = keep.tile([P, J // 16], U16, name="offsets")
@@ -42,27 +42,29 @@ def tile_list_feature_match_back_kernel(
         xs_all = keep.tile([P, T], U8, name="xs_all", align_bytes=64)
         wt_plane = keep.tile([P, K], U8, name="wt_plane", align_bytes=64)
         us_sb = keep.tile([P, PACK], F32, name="us_sb")
-        warm = keep.tile([P, 1], F32, name="warm")
-        warm2 = keep.tile([P, 1], F32, name="warm2")
 
-        nc.gpsimd.memset(ws_raw[:].bitcast(I32), 0)
         nc.vector.memset(xs_all[:].bitcast(I32), 0)
-        nc.vector.memset(warm[:], 0.0)
+        nc.gpsimd.memset(ws_raw[:].bitcast(I32), 0)
 
         tea_rows = tea.rearrange("(p t) c -> t p c", t=PACK)
+        tea_sb = [keep.tile([P, T], F32, name=f"tea{t}") for t in range(PACK)]
+        x_all = keep.tile([P, T], I32, name="x_all", align_bytes=64)
+        wt_codes = keep.tile([P, K], I32, name="wt_codes", align_bytes=64)
+        res_sb = [keep.tile([P, 2, J], F32, name=f"res{h}") for h in range(2)]
         nc.sync.dma_start(offsets[:], offs)
         nc.sync.dma_start(out=w_raw[:].bitcast(I32), in_=w_words[0].bitcast(I32))
-        load_scale_rows(nc.scalar, xs_all, xt_scales[0])
-        load_scale_rows(nc.gpsimd, ws_raw, w_scales[0])
-        nc.gpsimd.dma_start(out=us_sb[:], in_=us.rearrange("(p t) o -> p (t o)", t=PACK))
-        load_scale_rows(nc.gpsimd, wt_plane, wt_scales[0])
-        nc.scalar.activation(warm2[:], warm[:], ACT.Tanh)
-        x_all = ring.tile([P, T], I32, name="x_all", tag="big", align_bytes=64)
+        nc.sync.dma_start(out=us_sb[:], in_=us.rearrange("(p t) o -> p (t o)", t=PACK))
         nc.sync.dma_start(out=x_all[:], in_=xt_words[0].rearrange("p c r -> p (c r)").bitcast(I32))
-        tea_sb = []
-        for t in range(PACK - 1):
-            tea_sb.append(ring.tile([P, T], F32, name=f"tea{t}", tag="big", align_bytes=64))
+        load_scale_rows(nc, xs_all, xt_scales[0])
+        nc.sync.dma_start(out=tea_sb[0][:], in_=tea_rows[0])
+        load_scale_rows(nc, ws_raw, w_scales[0])
+        for t in range(1, PACK):
             nc.sync.dma_start(out=tea_sb[t][:], in_=tea_rows[t])
+        load_scale_rows(nc, wt_plane, wt_scales[0])
+        nc.sync.dma_start(out=wt_codes[:], in_=wt_words[0].rearrange("p c r -> p (c r)").bitcast(I32))
+        res_blocks = res.rearrange("(h b p) j -> h p b j", p=P, b=2)
+        for h in range(2):
+            nc.sync.dma_start(out=res_sb[h][:], in_=res_blocks[h])
 
         w_codes = keep.tile([P, 2 * N], U8, name="w_codes", align_bytes=64)
         w_plane = keep.tile([P, N], U8, name="w_plane", align_bytes=64)
@@ -70,47 +72,46 @@ def tile_list_feature_match_back_kernel(
             out=w_codes[:].bitcast(U16).rearrange("p (t m) -> p t m", t=PACK),
             in_=w_raw[:].bitcast(U16).rearrange("p (m t) -> p t m", t=PACK),
         )
+        neg_us = keep.tile([P, PACK], F32, name="neg_us")
+        nc.vector.tensor_scalar(neg_us[:], us_sb[:], -1.0, None, ALU.mult)
         x_codes = keep.tile([P, J], U32, name="x_codes", align_bytes=64)
         x_plane = keep.tile([P, J], U8, name="x_plane", align_bytes=64)
-        nc.vector.tensor_copy(x_codes[:], x_all[:].bitcast(U32).indirect(offsets[:]))
-        nc.vector.tensor_copy(x_plane[:], xs_all[:].indirect(offsets[:]))
+        for lo, hi in ((0, HALF), (HALF, J)):
+            entries = offsets[:, lo // 16 : hi // 16]
+            nc.vector.tensor_copy(x_codes[:, lo:hi], x_all[:].bitcast(U32).indirect(entries))
+            nc.vector.tensor_copy(x_plane[:, lo:hi], xs_all[:].indirect(entries))
         ws_by_slot = ws_raw[:].rearrange("p (m t) -> p t m", t=PACK)
         for t in range(PACK):
             nc.vector.tensor_copy(out=w_plane[:, P * t : P * (t + 1)], in_=ws_by_slot[:, t, :])
-        tea_sb.append(ring.tile([P, T], F32, name="tea3", tag="big", align_bytes=64))
-        nc.sync.dma_start(out=tea_sb[3][:], in_=tea_rows[3])
-        neg_us = keep.tile([P, PACK], F32, name="neg_us")
-        nc.gpsimd.tensor_scalar(neg_us[:], us_sb[:], -1.0, 0.0, ALU.mult, ALU.add)
 
         d_lo = keep.tile([P, HALF, PACK], BF16, name="d_lo", align_bytes=64)
         d_hi = keep.tile([P, HALF, PACK], BF16, name="d_hi", align_bytes=64)
         for t in range(PACK):
-            z = psum.tile([P, J], F32, name=f"z{t}")
-            nc.tensor.matmul_mx(
-                out=z[:],
-                lhsT=w_codes[:, 2 * P * t : 2 * P * (t + 1)].bitcast(E2M1),
-                lhsT_scale=w_plane[:, P * t : P * (t + 1)],
-                rhs=x_codes[:].bitcast(E4M3),
-                rhs_scale=x_plane[:],
-                start=True,
-                stop=True,
-            )
             th = keep.tile([P, J], F32, name=f"th{t}")
-            nc.scalar.activation(th[:], z[:], ACT.Tanh)
-            cuts = [0, J] if t < PACK - 1 else [0, HALF, HALF + HALF // 2, J]
+            cuts = [0, HALF, J] if t == 0 else [0, J]
+            for lo, hi in zip(cuts, cuts[1:]):
+                z = psum.tile([P, hi - lo], F32, name="z", tag="bank", bufs=8)
+                nc.tensor.matmul_mx(
+                    out=z[:],
+                    lhsT=w_codes[:, 2 * P * t : 2 * P * (t + 1)].bitcast(E2M1),
+                    lhsT_scale=w_plane[:, P * t : P * (t + 1)],
+                    rhs=x_codes[:, lo:hi].bitcast(E4M3),
+                    rhs_scale=x_plane[:, lo:hi],
+                    start=True,
+                    stop=True,
+                )
+                nc.scalar.activation(th[:, lo:hi], z[:], ACT.Tanh)
+            if t == PACK - 1:
+                cuts = [0, HALF, HALF + HALF // 2, J]
             diff = keep.tile([P, J], F32, name=f"diff{t}")
             for lo, hi in zip(cuts, cuts[1:]):
                 picked = tea_sb[t][:].indirect(offsets[:, lo // 16 : hi // 16])
                 nc.vector.tensor_tensor(diff[:, lo:hi], picked, th[:, lo:hi], ALU.subtract)
-            if t == 0:
-                wt_codes = ring.tile([P, K], I32, name="wt_codes", tag="big", align_bytes=64)
-                nc.sync.dma_start(out=wt_codes[:], in_=wt_words[0].rearrange("p c r -> p (c r)").bitcast(I32))
-            if t == 1:
-                res_sb = ring.tile([P, PACK, J], F32, name="res_sb", tag="big", align_bytes=64)
-                nc.sync.dma_start(out=res_sb[:], in_=res.rearrange("(b p) j -> p b j", p=P))
             factor = neg_us[:, t : t + 1]
             nc.scalar.activation(d_lo[:, :, t], diff[:, :HALF], ACT.Copy, scale=factor)
-            cuts = [HALF, J] if t < PACK - 1 else cuts[1:]
+            if t < 2:
+                nc.scalar.activation(d_hi[:, :QUARTER, t], diff[:, HALF : HALF + QUARTER], ACT.Copy, scale=factor)
+            cuts = [[HALF + QUARTER, J], [HALF + QUARTER, J], [HALF, J], cuts[1:]][t]
             for lo, hi in zip(cuts, cuts[1:]):
                 nc.vector.tensor_scalar(d_hi[:, lo - HALF : hi - HALF, t], diff[:, lo:hi], factor, None, ALU.mult)
 
@@ -122,7 +123,7 @@ def tile_list_feature_match_back_kernel(
                 out=d_codes[:, cols].bitcast(E5M2), scales=d_plane[:, cols], in_=d_half[:].rearrange("p j t -> p (j t)")
             )
         for b in range(PACK):
-            dx = psum.tile([P, J], F32, name=f"dx{b}")
+            dx = psum.tile([P, J], F32, name="dx", tag="bank", bufs=8)
             nc.tensor.matmul_mx(
                 out=dx[:],
                 lhsT=wt_codes[:, P * b : P * (b + 1)].bitcast(E4M3),
@@ -133,8 +134,8 @@ def tile_list_feature_match_back_kernel(
                 stop=True,
             )
             y = keep.tile([P, J], F32, name=f"y{b}")
-            cuts = [0, J] if b < PACK - 1 else [0, HALF, J]
+            cuts = [0, HALF, J] if b in (0, PACK - 1) else [0, J]
             for i, (lo, hi) in enumerate(zip(cuts, cuts[1:])):
-                nc.vector.tensor_tensor(y[:, lo:hi], dx[:, lo:hi], res_sb[:, b, lo:hi], ALU.add)
+                nc.vector.tensor_tensor(y[:, lo:hi], dx[:, lo:hi], res_sb[b // 2][:, b % 2, lo:hi], ALU.add)
                 queue = nc.sync if (b + i) % 2 == 0 else nc.scalar
                 queue.dma_start(out=out[P * b : P * (b + 1), lo:hi], in_=y[:, lo:hi])

@@ -18,79 +18,93 @@ ACT = mybir.ActivationFunctionType
 ALU = mybir.AluOpType
 
 P = 128
-PACK = 4
+SLOTS = 4
+QUADRANT = 32
+SCALE_ROWS = 4
+PER_COLUMN = 16
+BANKS = 8
+K_TILES = K // P
+RES_TILES = 2
 HALF = J // 2
-QUARTER = J // 4
+
+WHOLE = ((0, J),)
+HALVES = ((0, HALF), (HALF, J))
+UPPER_QUARTERS = ((HALF, HALF + J // 4), (HALF + J // 4, J))
 
 
-def load_scale_rows(nc, plane, rows):
-    for q in range(4):
-        nc.sync.dma_start(out=plane[32 * q : 32 * q + 4, :].bitcast(I32), in_=rows[4 * q : 4 * q + 4, :].bitcast(I32))
+def load_scale_plane(nc, plane, rows):
+    for r in range(SCALE_ROWS):
+        nc.sync.dma_start(out=plane[r:P:QUADRANT, :].bitcast(I32), in_=rows[r::SCALE_ROWS, :].bitcast(I32))
 
 
 def tile_list_feature_match_back_kernel(
     tc, xt_words, xt_scales, w_words, w_scales, tea, us, wt_words, wt_scales, res, offs, out
 ):
     nc = tc.nc
+    last_slot = SLOTS - 1
     with ExitStack() as ctx:
         keep = ctx.enter_context(tc.tile_pool(name="keep", bufs=1))
         psum = ctx.enter_context(tc.psum_pool(name="psum", bufs=1))
 
-        offsets = keep.tile([P, J // 16], U16, name="offsets")
+        offsets = keep.tile([P, J // PER_COLUMN], U16, name="offsets")
         w_raw = keep.tile([P, 2 * N], U8, name="w_raw", align_bytes=64)
-        ws_raw = keep.tile([P, N], U8, name="ws_raw", align_bytes=64)
-        xs_all = keep.tile([P, T], U8, name="xs_all", align_bytes=64)
+        w_plane_raw = keep.tile([P, N], U8, name="w_plane_raw", align_bytes=64)
+        xt_plane = keep.tile([P, T], U8, name="xt_plane", align_bytes=64)
         wt_plane = keep.tile([P, K], U8, name="wt_plane", align_bytes=64)
-        us_sb = keep.tile([P, PACK], F32, name="us_sb")
+        us_sb = keep.tile([P, SLOTS], F32, name="us_sb")
 
-        nc.vector.memset(xs_all[:].bitcast(I32), 0)
-        nc.gpsimd.memset(ws_raw[:].bitcast(I32), 0)
+        def entries(lo, hi):
+            return offsets[:, lo // PER_COLUMN : hi // PER_COLUMN]
 
-        tea_rows = tea.rearrange("(p t) c -> t p c", t=PACK)
-        tea_sb = [keep.tile([P, T], F32, name=f"tea{t}") for t in range(PACK)]
-        x_all = keep.tile([P, T], I32, name="x_all", align_bytes=64)
+        nc.vector.memset(xt_plane[:].bitcast(I32), 0)
+        nc.gpsimd.memset(w_plane_raw[:].bitcast(I32), 0)
+
+        tea_rows = tea.rearrange("(p t) c -> t p c", t=SLOTS)
+        tea_sb = [keep.tile([P, T], F32, name=f"tea{t}") for t in range(SLOTS)]
+        xt_sb = keep.tile([P, T], I32, name="xt_sb", align_bytes=64)
         wt_codes = keep.tile([P, K], I32, name="wt_codes", align_bytes=64)
-        res_sb = [keep.tile([P, 2, J], F32, name=f"res{h}") for h in range(2)]
+        res_sb = [keep.tile([P, RES_TILES, J], F32, name=f"res{h}") for h in range(K_TILES // RES_TILES)]
         nc.sync.dma_start(offsets[:], offs)
         nc.sync.dma_start(out=w_raw[:].bitcast(I32), in_=w_words[0].bitcast(I32))
-        nc.sync.dma_start(out=us_sb[:], in_=us.rearrange("(p t) o -> p (t o)", t=PACK))
-        nc.sync.dma_start(out=x_all[:], in_=xt_words[0].rearrange("p c r -> p (c r)").bitcast(I32))
-        load_scale_rows(nc, xs_all, xt_scales[0])
+        nc.sync.dma_start(out=us_sb[:], in_=us.rearrange("(p t) o -> p (t o)", t=SLOTS))
+        nc.sync.dma_start(out=xt_sb[:], in_=xt_words[0].rearrange("p c r -> p (c r)").bitcast(I32))
+        load_scale_plane(nc, xt_plane, xt_scales[0])
         nc.sync.dma_start(out=tea_sb[0][:], in_=tea_rows[0])
-        load_scale_rows(nc, ws_raw, w_scales[0])
-        for t in range(1, PACK):
+        load_scale_plane(nc, w_plane_raw, w_scales[0])
+        for t in range(1, SLOTS):
             nc.sync.dma_start(out=tea_sb[t][:], in_=tea_rows[t])
-        load_scale_rows(nc, wt_plane, wt_scales[0])
+        load_scale_plane(nc, wt_plane, wt_scales[0])
         nc.sync.dma_start(out=wt_codes[:], in_=wt_words[0].rearrange("p c r -> p (c r)").bitcast(I32))
-        res_blocks = res.rearrange("(h b p) j -> h p b j", p=P, b=2)
-        for h in range(2):
-            nc.sync.dma_start(out=res_sb[h][:], in_=res_blocks[h])
+        res_parts = res.rearrange("(h b p) j -> h p b j", p=P, b=RES_TILES)
+        for h, part in enumerate(res_sb):
+            nc.sync.dma_start(out=part[:], in_=res_parts[h])
 
         w_codes = keep.tile([P, 2 * N], U8, name="w_codes", align_bytes=64)
         w_plane = keep.tile([P, N], U8, name="w_plane", align_bytes=64)
         nc.vector.tensor_copy(
-            out=w_codes[:].bitcast(U16).rearrange("p (t m) -> p t m", t=PACK),
-            in_=w_raw[:].bitcast(U16).rearrange("p (m t) -> p t m", t=PACK),
+            out=w_codes[:].bitcast(U16).rearrange("p (t m) -> p t m", t=SLOTS),
+            in_=w_raw[:].bitcast(U16).rearrange("p (m t) -> p t m", t=SLOTS),
         )
-        neg_us = keep.tile([P, PACK], F32, name="neg_us")
+        neg_us = keep.tile([P, SLOTS], F32, name="neg_us")
         nc.vector.tensor_scalar(neg_us[:], us_sb[:], -1.0, None, ALU.mult)
+
         x_codes = keep.tile([P, J], U32, name="x_codes", align_bytes=64)
         x_plane = keep.tile([P, J], U8, name="x_plane", align_bytes=64)
-        for lo, hi in ((0, HALF), (HALF, J)):
-            entries = offsets[:, lo // 16 : hi // 16]
-            nc.vector.tensor_copy(x_codes[:, lo:hi], x_all[:].bitcast(U32).indirect(entries))
-            nc.vector.tensor_copy(x_plane[:, lo:hi], xs_all[:].indirect(entries))
-        ws_by_slot = ws_raw[:].rearrange("p (m t) -> p t m", t=PACK)
-        for t in range(PACK):
-            nc.vector.tensor_copy(out=w_plane[:, P * t : P * (t + 1)], in_=ws_by_slot[:, t, :])
+        for lo, hi in HALVES:
+            nc.vector.tensor_copy(x_codes[:, lo:hi], xt_sb[:].bitcast(U32).indirect(entries(lo, hi)))
+            nc.vector.tensor_copy(x_plane[:, lo:hi], xt_plane[:].indirect(entries(lo, hi)))
+        w_plane_by_slot = w_plane_raw[:].rearrange("p (m t) -> p t m", t=SLOTS)
+        for t in range(SLOTS):
+            nc.vector.tensor_copy(out=w_plane[:, P * t : P * (t + 1)], in_=w_plane_by_slot[:, t, :])
 
-        d_lo = keep.tile([P, HALF, PACK], BF16, name="d_lo", align_bytes=64)
-        d_hi = keep.tile([P, HALF, PACK], BF16, name="d_hi", align_bytes=64)
-        for t in range(PACK):
-            th = keep.tile([P, J], F32, name=f"th{t}")
-            cuts = [0, HALF, J] if t == 0 else [0, J]
-            for lo, hi in zip(cuts, cuts[1:]):
-                z = psum.tile([P, hi - lo], F32, name="z", tag="bank", bufs=8)
+        d_lower = keep.tile([P, HALF, SLOTS], BF16, name="d_lower", align_bytes=64)
+        d_upper = keep.tile([P, HALF, SLOTS], BF16, name="d_upper", align_bytes=64)
+        tanh_z = []
+        for t in range(SLOTS):
+            tanh_t = keep.tile([P, J], F32, name=f"tanh{t}")
+            tanh_z.append(tanh_t)
+            for lo, hi in HALVES if t == 0 else WHOLE:
+                z = psum.tile([P, hi - lo], F32, name="z", tag="bank", bufs=BANKS)
                 nc.tensor.matmul_mx(
                     out=z[:],
                     lhsT=w_codes[:, 2 * P * t : 2 * P * (t + 1)].bitcast(E2M1),
@@ -100,42 +114,53 @@ def tile_list_feature_match_back_kernel(
                     start=True,
                     stop=True,
                 )
-                nc.scalar.activation(th[:, lo:hi], z[:], ACT.Tanh)
-            if t == PACK - 1:
-                cuts = [0, HALF, HALF + HALF // 2, J]
+                nc.scalar.activation(tanh_t[:, lo:hi], z[:], ACT.Tanh)
+
+        gather_pieces = {0: HALVES, last_slot: HALVES[:1] + UPPER_QUARTERS}
+        diffs = []
+        for t, tanh_t in enumerate(tanh_z):
             diff = keep.tile([P, J], F32, name=f"diff{t}")
-            for lo, hi in zip(cuts, cuts[1:]):
-                picked = tea_sb[t][:].indirect(offsets[:, lo // 16 : hi // 16])
-                nc.vector.tensor_tensor(diff[:, lo:hi], picked, th[:, lo:hi], ALU.subtract)
+            diffs.append(diff)
+            for lo, hi in gather_pieces.get(t, WHOLE):
+                picked = tea_sb[t][:].indirect(entries(lo, hi))
+                nc.vector.tensor_tensor(diff[:, lo:hi], picked, tanh_t[:, lo:hi], ALU.subtract)
+
+        for t, diff in enumerate(diffs):
             factor = neg_us[:, t : t + 1]
-            nc.scalar.activation(d_lo[:, :, t], diff[:, :HALF], ACT.Copy, scale=factor)
-            if t < 2:
-                nc.scalar.activation(d_hi[:, :QUARTER, t], diff[:, HALF : HALF + QUARTER], ACT.Copy, scale=factor)
-            cuts = [[HALF + QUARTER, J], [HALF + QUARTER, J], [HALF, J], cuts[1:]][t]
-            for lo, hi in zip(cuts, cuts[1:]):
-                nc.vector.tensor_scalar(d_hi[:, lo - HALF : hi - HALF, t], diff[:, lo:hi], factor, None, ALU.mult)
+            first_pair = t < SLOTS // 2
+            if first_pair:
+                nc.scalar.activation(d_upper[:, :, t], diff[:, HALF:], ACT.Copy, scale=factor)
+            nc.scalar.activation(d_lower[:, :, t], diff[:, :HALF], ACT.Copy, scale=factor)
+            if not first_pair:
+                for lo, hi in UPPER_QUARTERS if t == last_slot else HALVES[1:]:
+                    nc.vector.tensor_scalar(
+                        d_upper[:, lo - HALF : hi - HALF, t], diff[:, lo:hi], factor, None, ALU.mult
+                    )
 
         d_codes = keep.tile([P, J], U32, name="d_codes", align_bytes=64)
         d_plane = keep.tile([P, J], U8, name="d_plane", align_bytes=64)
-        for h, d_half in enumerate((d_lo, d_hi)):
-            cols = slice(HALF * h, HALF * (h + 1))
+        for (lo, hi), d_half in zip(HALVES, (d_lower, d_upper)):
             nc.vector.quantize_mx(
-                out=d_codes[:, cols].bitcast(E5M2), scales=d_plane[:, cols], in_=d_half[:].rearrange("p j t -> p (j t)")
+                out=d_codes[:, lo:hi].bitcast(E5M2),
+                scales=d_plane[:, lo:hi],
+                in_=d_half[:].rearrange("p j t -> p (j t)"),
             )
-        for b in range(PACK):
-            dx = psum.tile([P, J], F32, name="dx", tag="bank", bufs=8)
+
+        for b in range(K_TILES):
+            rows = slice(P * b, P * (b + 1))
+            dx = psum.tile([P, J], F32, name="dx", tag="bank", bufs=BANKS)
             nc.tensor.matmul_mx(
                 out=dx[:],
-                lhsT=wt_codes[:, P * b : P * (b + 1)].bitcast(E4M3),
-                lhsT_scale=wt_plane[:, P * b : P * (b + 1)],
+                lhsT=wt_codes[:, rows].bitcast(E4M3),
+                lhsT_scale=wt_plane[:, rows],
                 rhs=d_codes[:].bitcast(E5M2),
                 rhs_scale=d_plane[:],
                 start=True,
                 stop=True,
             )
             y = keep.tile([P, J], F32, name=f"y{b}")
-            cuts = [0, HALF, J] if b in (0, PACK - 1) else [0, J]
-            for i, (lo, hi) in enumerate(zip(cuts, cuts[1:])):
-                nc.vector.tensor_tensor(y[:, lo:hi], dx[:, lo:hi], res_sb[b // 2][:, b % 2, lo:hi], ALU.add)
+            res_tile = res_sb[b // RES_TILES][:, b % RES_TILES, :]
+            for i, (lo, hi) in enumerate(HALVES if b in (0, K_TILES - 1) else WHOLE):
+                nc.vector.tensor_tensor(y[:, lo:hi], dx[:, lo:hi], res_tile[:, lo:hi], ALU.add)
                 queue = nc.sync if (b + i) % 2 == 0 else nc.scalar
-                queue.dma_start(out=out[P * b : P * (b + 1), lo:hi], in_=y[:, lo:hi])
+                queue.dma_start(out=out[rows, lo:hi], in_=y[:, lo:hi])

from contextlib import ExitStack

import concourse.mybir as mybir

K, N, T, J = 512, 512, 2048, 512
FLOPS = 2 * 2 * K * N * J

F32 = mybir.dt.float32
BF16 = mybir.dt.bfloat16
I32 = mybir.dt.int32
U32 = mybir.dt.uint32
U16 = mybir.dt.uint16
U8 = mybir.dt.uint8
E4M3 = mybir.dt.float8_e4m3fn_x4
E5M2 = mybir.dt.float8_e5m2_x4
E2M1 = mybir.dt.float4_e2m1fn_x4
ACT = mybir.ActivationFunctionType
ALU = mybir.AluOpType

P = 128
SLOTS = 4
QUADRANT = 32
SCALE_ROWS = 4
PER_COLUMN = 16
BANKS = 8
K_TILES = K // P
RES_TILES = 2
HALF = J // 2

WHOLE = ((0, J),)
HALVES = ((0, HALF), (HALF, J))
UPPER_QUARTERS = ((HALF, HALF + J // 4), (HALF + J // 4, J))


def load_scale_plane(nc, plane, rows):
    for r in range(SCALE_ROWS):
        nc.sync.dma_start(out=plane[r:P:QUADRANT, :].bitcast(I32), in_=rows[r::SCALE_ROWS, :].bitcast(I32))


def tile_list_feature_match_back_kernel(
    tc, xt_words, xt_scales, w_words, w_scales, tea, us, wt_words, wt_scales, res, offs, out
):
    nc = tc.nc
    last_slot = SLOTS - 1
    with ExitStack() as ctx:
        keep = ctx.enter_context(tc.tile_pool(name="keep", bufs=1))
        psum = ctx.enter_context(tc.psum_pool(name="psum", bufs=1))

        offsets = keep.tile([P, J // PER_COLUMN], U16, name="offsets")
        w_raw = keep.tile([P, 2 * N], U8, name="w_raw", align_bytes=64)
        w_plane_raw = keep.tile([P, N], U8, name="w_plane_raw", align_bytes=64)
        xt_plane = keep.tile([P, T], U8, name="xt_plane", align_bytes=64)
        wt_plane = keep.tile([P, K], U8, name="wt_plane", align_bytes=64)
        us_sb = keep.tile([P, SLOTS], F32, name="us_sb")

        def entries(lo, hi):
            return offsets[:, lo // PER_COLUMN : hi // PER_COLUMN]

        nc.vector.memset(xt_plane[:].bitcast(I32), 0)
        nc.gpsimd.memset(w_plane_raw[:].bitcast(I32), 0)

        tea_rows = tea.rearrange("(p t) c -> t p c", t=SLOTS)
        tea_sb = [keep.tile([P, T], F32, name=f"tea{t}") for t in range(SLOTS)]
        xt_sb = keep.tile([P, T], I32, name="xt_sb", align_bytes=64)
        wt_codes = keep.tile([P, K], I32, name="wt_codes", align_bytes=64)
        res_sb = [keep.tile([P, RES_TILES, J], F32, name=f"res{h}") for h in range(K_TILES // RES_TILES)]
        nc.sync.dma_start(offsets[:], offs)
        nc.sync.dma_start(out=w_raw[:].bitcast(I32), in_=w_words[0].bitcast(I32))
        nc.sync.dma_start(out=us_sb[:], in_=us.rearrange("(p t) o -> p (t o)", t=SLOTS))
        nc.sync.dma_start(out=xt_sb[:], in_=xt_words[0].rearrange("p c r -> p (c r)").bitcast(I32))
        load_scale_plane(nc, xt_plane, xt_scales[0])
        nc.sync.dma_start(out=tea_sb[0][:], in_=tea_rows[0])
        load_scale_plane(nc, w_plane_raw, w_scales[0])
        for t in range(1, SLOTS):
            nc.sync.dma_start(out=tea_sb[t][:], in_=tea_rows[t])
        load_scale_plane(nc, wt_plane, wt_scales[0])
        nc.sync.dma_start(out=wt_codes[:], in_=wt_words[0].rearrange("p c r -> p (c r)").bitcast(I32))
        res_parts = res.rearrange("(h b p) j -> h p b j", p=P, b=RES_TILES)
        for h, part in enumerate(res_sb):
            nc.sync.dma_start(out=part[:], in_=res_parts[h])

        w_codes = keep.tile([P, 2 * N], U8, name="w_codes", align_bytes=64)
        w_plane = keep.tile([P, N], U8, name="w_plane", align_bytes=64)
        nc.vector.tensor_copy(
            out=w_codes[:].bitcast(U16).rearrange("p (t m) -> p t m", t=SLOTS),
            in_=w_raw[:].bitcast(U16).rearrange("p (m t) -> p t m", t=SLOTS),
        )
        neg_us = keep.tile([P, SLOTS], F32, name="neg_us")
        nc.vector.tensor_scalar(neg_us[:], us_sb[:], -1.0, None, ALU.mult)

        x_codes = keep.tile([P, J], U32, name="x_codes", align_bytes=64)
        x_plane = keep.tile([P, J], U8, name="x_plane", align_bytes=64)
        for lo, hi in HALVES:
            nc.vector.tensor_copy(x_codes[:, lo:hi], xt_sb[:].bitcast(U32).indirect(entries(lo, hi)))
            nc.vector.tensor_copy(x_plane[:, lo:hi], xt_plane[:].indirect(entries(lo, hi)))
        w_plane_by_slot = w_plane_raw[:].rearrange("p (m t) -> p t m", t=SLOTS)
        for t in range(SLOTS):
            nc.vector.tensor_copy(out=w_plane[:, P * t : P * (t + 1)], in_=w_plane_by_slot[:, t, :])

        d_lower = keep.tile([P, HALF, SLOTS], BF16, name="d_lower", align_bytes=64)
        d_upper = keep.tile([P, HALF, SLOTS], BF16, name="d_upper", align_bytes=64)
        tanh_z = []
        for t in range(SLOTS):
            tanh_t = keep.tile([P, J], F32, name=f"tanh{t}")
            tanh_z.append(tanh_t)
            for lo, hi in HALVES if t == 0 else WHOLE:
                z = psum.tile([P, hi - lo], F32, name="z", tag="bank", bufs=BANKS)
                nc.tensor.matmul_mx(
                    out=z[:],
                    lhsT=w_codes[:, 2 * P * t : 2 * P * (t + 1)].bitcast(E2M1),
                    lhsT_scale=w_plane[:, P * t : P * (t + 1)],
                    rhs=x_codes[:, lo:hi].bitcast(E4M3),
                    rhs_scale=x_plane[:, lo:hi],
                    start=True,
                    stop=True,
                )
                nc.scalar.activation(tanh_t[:, lo:hi], z[:], ACT.Tanh)

        gather_pieces = {0: HALVES, last_slot: HALVES[:1] + UPPER_QUARTERS}
        diffs = []
        for t, tanh_t in enumerate(tanh_z):
            diff = keep.tile([P, J], F32, name=f"diff{t}")
            diffs.append(diff)
            for lo, hi in gather_pieces.get(t, WHOLE):
                picked = tea_sb[t][:].indirect(entries(lo, hi))
                nc.vector.tensor_tensor(diff[:, lo:hi], picked, tanh_t[:, lo:hi], ALU.subtract)

        for t, diff in enumerate(diffs):
            factor = neg_us[:, t : t + 1]
            first_pair = t < SLOTS // 2
            if first_pair:
                nc.scalar.activation(d_upper[:, :, t], diff[:, HALF:], ACT.Copy, scale=factor)
            nc.scalar.activation(d_lower[:, :, t], diff[:, :HALF], ACT.Copy, scale=factor)
            if not first_pair:
                for lo, hi in UPPER_QUARTERS if t == last_slot else HALVES[1:]:
                    nc.vector.tensor_scalar(
                        d_upper[:, lo - HALF : hi - HALF, t], diff[:, lo:hi], factor, None, ALU.mult
                    )

        d_codes = keep.tile([P, J], U32, name="d_codes", align_bytes=64)
        d_plane = keep.tile([P, J], U8, name="d_plane", align_bytes=64)
        for (lo, hi), d_half in zip(HALVES, (d_lower, d_upper)):
            nc.vector.quantize_mx(
                out=d_codes[:, lo:hi].bitcast(E5M2),
                scales=d_plane[:, lo:hi],
                in_=d_half[:].rearrange("p j t -> p (j t)"),
            )

        for b in range(K_TILES):
            rows = slice(P * b, P * (b + 1))
            dx = psum.tile([P, J], F32, name="dx", tag="bank", bufs=BANKS)
            nc.tensor.matmul_mx(
                out=dx[:],
                lhsT=wt_codes[:, rows].bitcast(E4M3),
                lhsT_scale=wt_plane[:, rows],
                rhs=d_codes[:].bitcast(E5M2),
                rhs_scale=d_plane[:],
                start=True,
                stop=True,
            )
            y = keep.tile([P, J], F32, name=f"y{b}")
            res_tile = res_sb[b // RES_TILES][:, b % RES_TILES, :]
            for i, (lo, hi) in enumerate(HALVES if b in (0, K_TILES - 1) else WHOLE):
                nc.vector.tensor_tensor(y[:, lo:hi], dx[:, lo:hi], res_tile[:, lo:hi], ALU.add)
                queue = nc.sync if (b + i) % 2 == 0 else nc.scalar
                queue.dma_start(out=out[rows, lo:hi], in_=y[:, lo:hi])
